import numpy as np
import ml_dtypes


def mxq(x, axis, fmt="e4m3"):
    dtype, down = {"e4m3": (ml_dtypes.float8_e4m3fn, 7), "e5m2": (ml_dtypes.float8_e5m2, 14)}[fmt]
    v = np.moveaxis(np.asarray(x, np.float32).astype(ml_dtypes.bfloat16).astype(np.float64), axis, -1)
    blocks = v.reshape(v.shape[:-1] + (-1, 32))
    amax = np.abs(blocks).max(-1, keepdims=True)
    byte = np.maximum(np.where(amax > 0, np.frexp(amax)[1] - 1 + 127, 0) - down, 1)
    scale = np.exp2(byte - 127.0)
    codes = (blocks / scale).astype(np.float32).astype(dtype).astype(np.float64)
    return np.moveaxis((codes * scale).reshape(v.shape), -1, axis)


WIDE = False


def mx_kscale(k):
    if not WIDE:
        return np.ones(k)
    levels = np.array([10, -10, 5, -5, 0])
    if k % 512:
        return np.exp2(np.random.permutation(np.resize(levels, k // 32))).repeat(32)
    a = np.empty((k // 512, 16))
    for p in range(k // 512):
        a[p, :8] = np.random.permutation(np.resize(levels, 8))
        for g in range(8):
            far = levels[np.abs(levels - a[p, g]) >= 10]
            a[p, g + 8] = far[np.random.randint(len(far))]
    return np.exp2(a.ravel()).repeat(32)


def f64(x):
    return np.asarray(x).astype(np.float64)


def striped(idx):
    return np.tile(idx.reshape(-1, 16).T, (8, 1)).astype(np.uint16)


def unstriped(offs):
    return offs[:16].T.reshape(-1).astype(np.int64)


E2M1 = np.array([0.0, 0.5, 1.0, 1.5, 2.0, 3.0, 4.0, 6.0, -0.0, -0.5, -1.0, -1.5, -2.0, -3.0, -4.0, -6.0])


def pack_weight(w, fmt):
    k, n = w.shape
    w = f64(np.asarray(w, np.float32).astype(ml_dtypes.bfloat16)).reshape(k // 32, 32, n)
    amax = np.abs(w).max(1)
    if fmt == "e4m3":
        byte = np.frexp(amax)[1] - 1 + 127 - 7
    else:
        mant, ex = np.frexp(amax / 6.0)
        byte = np.where(mant > 0.5, ex, ex - 1) + 127
    byte = np.clip(np.where(amax > 0, byte, 1), 1, 254)
    scaled = (w * np.exp2(127.0 - byte)[:, None, :]).reshape(k, n).astype(np.float32)
    by_word = np.ascontiguousarray(scaled.reshape(k // 512, 128, 4, n).transpose(0, 1, 3, 2))
    if fmt == "e4m3":
        words = by_word.astype(ml_dtypes.float8_e4m3fn).view(np.uint8)
    else:
        c = by_word.astype(ml_dtypes.float4_e2m1fn).view(np.uint8) & 0xF
        words = (c[..., 0::2] | (c[..., 1::2] << 4)).reshape(k // 512, 128, 2 * n)
    return np.ascontiguousarray(words), np.ascontiguousarray(byte.astype(np.uint8).reshape(k // 512, 16, n))


def unpack_weight(words, scales, fmt):
    g, _, n = scales.shape
    words = np.ascontiguousarray(words).reshape(g, 128, n, -1)
    if fmt == "e4m3":
        vals = words.view(ml_dtypes.float8_e4m3fn).astype(np.float64)
    else:
        nib = np.empty((g, 128, n, 4), np.uint8)
        nib[..., 0::2] = words & 0xF
        nib[..., 1::2] = words >> 4
        vals = E2M1[nib]
    vals = vals * np.repeat(np.exp2(scales.astype(np.float64) - 127.0), 8, axis=1)[..., None]
    return vals.transpose(0, 1, 3, 2).reshape(g * 512, n)


def sigmoid(v):
    return 1.0 / (1.0 + np.exp(-np.maximum(v, -700.0)))


K, T, E, C, H, N = 1024, 512, 8, 128, 512, 128


def by_expert(wq, xq):
    return np.concatenate([wq[e].T @ xq[:, e * C:(e + 1) * C] for e in range(E)], axis=1)


def setup_inputs():
    n = np.random.standard_normal
    s = mx_kscale(K)[:, None]
    u = mx_kscale(H)
    first = np.random.permutation(np.repeat(np.arange(E), T // E))
    second = (first + 1 + np.random.permutation(np.repeat(np.arange(E - 1), -(-T // (E - 1)))[:T])) % E
    while np.bincount(second, minlength=E).max() != T // E:
        load = np.bincount(second, minlength=E); hi, lo = int(load.argmax()), int(load.argmin())
        t = np.flatnonzero((second == hi) & (first != lo))[0]; second[t] = lo
    slot_token = np.empty(E * C, np.int64); pos = np.empty((2, T), np.int64); fill = np.zeros(E, np.int64)
    place = np.stack([np.random.permutation(C) for _ in range(E)])
    for r, deal in enumerate((first, second)):
        for t in np.random.permutation(T):
            e = deal[t]; j = e * C + place[e, fill[e]]; fill[e] += 1; slot_token[j] = t; pos[r, t] = j
    g = np.random.uniform(0.2, 0.8, T)
    x = pack_weight(n((K, T)) * s, "e4m3")
    return {
        "x_words": x[0],
        "x_scales": x[1],
        "w1": (n((E + 1, K, H)) / np.sqrt(K) / s[None]).astype(np.float32),
        "w3": (n((E + 1, K, H)) / np.sqrt(K) / s[None] * u[None, None, :]).astype(np.float32),
        "w2": (n((E + 1, H, N)) / np.sqrt(H) / u[None, :, None]).astype(np.float32),
        "gate": np.stack([np.tile(g, (N, 1)), np.tile(1.0 - g, (N, 1))]).astype(np.float32),
        "offs": striped(slot_token),
        "pos1": striped(pos[0]),
        "pos2": striped(pos[1]),
    }


def reference(x_words, x_scales, w1, w3, w2, gate, offs, pos1, pos2):
    idx = unstriped(offs)
    w1q, w3q, w2q = mxq(f64(w1), 1, "e4m3"), mxq(f64(w3), 1, "e4m3"), mxq(f64(w2), 1, "e4m3")
    xs = unpack_weight(x_words, x_scales, "e4m3")
    hs = sigmoid(w1q[E].T @ xs) * (w3q[E].T @ xs)
    ys = w2q[E].T @ mxq(hs, 0, "e4m3")
    xq = unpack_weight(x_words, x_scales, "e4m3")[:, idx]
    h = sigmoid(by_expert(w1q, xq))
    h = h * by_expert(w3q, xq)
    y = by_expert(w2q, mxq(h, 0, "e4m3"))
    return ys + f64(gate[0]) * y[:, unstriped(pos1)] + f64(gate[1]) * y[:, unstriped(pos2)]

@@ -1,0 +1,301 @@
+from contextlib import ExitStack
+
+import concourse.mybir as mybir
+from concourse.masks import make_identity
+
+K, T, E, C, H, N = 1024, 512, 8, 128, 512, 128
+FLOPS = 3422552064
+
+F32 = mybir.dt.float32
+BF16 = mybir.dt.bfloat16
+I32 = mybir.dt.int32
+U32 = mybir.dt.uint32
+U16 = mybir.dt.uint16
+U8 = mybir.dt.uint8
+FP8X4 = mybir.dt.float8_e4m3fn_x4
+MULT = mybir.AluOpType.mult
+ADD = mybir.AluOpType.add
+SIGMOID = mybir.ActivationFunctionType.Sigmoid
+
+P = 128
+PACK = 4
+K_PASS = P * PACK
+PASSES = K // K_PASS
+GATHER = 256
+RAW_BUFS = 8
+
+
+def tile_moe_shr_glu_sigmoid_kernel(
+    tc, x_words, x_scales, w1, w3, w2, gate, offs, pos1, pos2, out
+):
+    nc = tc.nc
+    with ExitStack() as ctx:
+        keep = ctx.enter_context(tc.tile_pool(name="keep", bufs=1))
+        ring = ctx.enter_context(tc.tile_pool(name="ring", bufs=1))
+        psum = ctx.enter_context(tc.psum_pool(name="psum", bufs=1))
+
+        def raw_tile(cols):
+            return ring.tile([P, cols], F32, name="raw", tag="raw", bufs=RAW_BUFS)
+
+        def load_matrix(w):
+            raw = raw_tile(PASSES * PACK * H)
+            nc.sync.dma_start(
+                out=raw[:].rearrange("p (o r) -> p o r", o=PASSES),
+                in_=w.rearrange("(o p j) c -> p o (j c)", o=PASSES, j=PACK),
+            )
+            return [raw[:, o * PACK * H:(o + 1) * PACK * H] for o in range(PASSES)]
+
+        def load_piece(w, o, c0, c1):
+            raw = raw_tile(PACK * (c1 - c0))
+            rows = w[o * K_PASS:(o + 1) * K_PASS, c0:c1]
+            nc.sync.dma_start(
+                out=raw[:].rearrange("p (j c) -> p j c", j=PACK),
+                in_=rows.rearrange("(p j) c -> p j c", j=PACK),
+            )
+            return raw[:]
+
+        def copy_on(engine, dst, src):
+            if engine == "scalar":
+                nc.scalar.copy(out=dst, in_=src)
+            else:
+                nc.vector.tensor_copy(out=dst, in_=src)
+
+        def stage_tile(o):
+            return ring.tile([P, PACK * H], BF16, name="stage%d" % o, tag="stage%d" % o, bufs=1, align_bytes=64)
+
+        def quantize_w(stage, o, pieces=1):
+            return quantize(stage, H, "w%d" % o, 1 + o, pieces)
+
+        def round_w(engine, stage, m0, m1, raw, raw_m0):
+            dst = stage[:].rearrange("p (t m j) -> p m j t", t=PACK, j=PACK)
+            src = raw.rearrange("p (j m t) -> p m j t", j=PACK, t=PACK)
+            copy_on(engine, dst[:, m0:m1], src[:, m0 - raw_m0:m1 - raw_m0])
+
+        def quantize(stage, words, tag, bufs, pieces=1):
+            codes = ring.tile([P, words], U32, name=tag + "_codes", tag=tag + "_codes", bufs=bufs, align_bytes=64)
+            scales = ring.tile([P, words], U8, name=tag + "_scales", tag=tag + "_scales", bufs=bufs, align_bytes=64)
+            step = words // pieces
+            for i in range(pieces):
+                nc.vector.quantize_mx(
+                    out=codes[:, i * step:(i + 1) * step].bitcast(FP8X4),
+                    scales=scales[:, i * step:(i + 1) * step],
+                    in_=stage[:, PACK * i * step:PACK * (i + 1) * step],
+                )
+            return codes, scales
+
+        def round_w2(engine, stage, raw, experts):
+            dst = stage.rearrange("p (e c i j) -> p e c j i", e=experts, i=4, j=PACK)
+            src = raw.rearrange("p (e j c i) -> p e c j i", e=experts, j=PACK, i=4)
+            copy_on(engine, dst, src)
+
+        def first_layer(wq, tokens, tag):
+            bank = psum.tile([P, PACK, C], F32, name=tag, tag=tag, bufs=3)
+            for t in range(PACK):
+                cols = slice(t * P, (t + 1) * P)
+                for o in range(PASSES):
+                    codes, scales = wq[o]
+                    words, bytes_ = tokens[o]
+                    nc.tensor.matmul_mx(
+                        out=bank[:, t, :],
+                        lhsT=codes[:, cols].bitcast(FP8X4),
+                        lhsT_scale=scales[:, cols],
+                        rhs=words.bitcast(FP8X4),
+                        rhs_scale=bytes_,
+                        start=(o == 0),
+                        stop=(o == PASSES - 1),
+                    )
+            return bank
+
+        def sigmoid_of(bank, place):
+            sig = place.rearrange("p (n t) -> p n t", t=PACK)
+            nc.scalar.activation(out=sig, in_=bank[:].rearrange("p t n -> p n t"), func=SIGMOID)
+            return sig
+
+        def gated(bank, sig, hidden):
+            nc.vector.tensor_tensor(
+                out=hidden.rearrange("p (n t) -> p n t", t=PACK),
+                in0=bank[:].rearrange("p t n -> p n t"),
+                in1=sig,
+                op=MULT,
+            )
+            return hidden
+
+        def second_layer(w2q, e, hq):
+            bank = psum.tile([P, C], F32, name="ybank", tag="ybank", bufs=2)
+            cols = slice(e * N, (e + 1) * N)
+            nc.tensor.matmul_mx(
+                out=bank[:],
+                lhsT=w2q[0][:, cols].bitcast(FP8X4),
+                lhsT_scale=w2q[1][:, cols],
+                rhs=hq[0][:].bitcast(FP8X4),
+                rhs_scale=hq[1][:],
+                start=True,
+                stop=True,
+            )
+            return bank
+
+        xs = keep.tile([P, T], U8, name="xs", align_bytes=64)
+        nc.vector.memset(xs[:].bitcast(I32), 0)
+        xw = keep.tile([P, PASSES * T], I32, name="xw", align_bytes=64)
+        nc.sync.dma_start(
+            out=xw[:].rearrange("p (o t) -> p o t", o=PASSES),
+            in_=x_words.rearrange("o p t r -> p o (t r)").bitcast(I32),
+        )
+        offs_sb = keep.tile([P, E * C // 16], U16, name="offs_sb")
+        nc.sync.dma_start(offs_sb[:], offs)
+        xs_rows = keep.tile([P, T // 4], I32, name="xs_rows")
+        for q in range(4):
+            nc.sync.dma_start(
+                out=xs_rows[32 * q:32 * q + 4 * PASSES, :],
+                in_=x_scales[:, 4 * q:4 * q + 4, :].bitcast(I32),
+            )
+        gate_row = keep.tile([P, 2, PACK], F32, name="gate_row")
+        nc.sync.dma_start(out=gate_row[:], in_=gate[:, 0, :].rearrange("r (p j) -> p r j", j=PACK))
+        raws = {0: load_matrix(w1[0]), 1: load_matrix(w3[0])}
+        for q in range(4):
+            rows = slice(32 * q, 32 * q + 4 * PASSES)
+            nc.vector.tensor_copy(out=xs[:].bitcast(I32)[rows, :], in_=xs_rows[rows, :])
+        raw_w2 = raw_tile(E * PACK * N)
+        nc.sync.dma_start(
+            out=raw_w2[:].rearrange("p (e r) -> p e r", e=E),
+            in_=w2[0:E].rearrange("e (p j) n -> p e (j n)", j=PACK),
+        )
+        raws[2] = load_matrix(w1[1])
+        pos1_sb = keep.tile([P, T // 16], U16, name="pos1_sb")
+        nc.sync.dma_start(pos1_sb[:], pos1)
+        pos2_sb = keep.tile([P, T // 16], U16, name="pos2_sb")
+        nc.sync.dma_start(pos2_sb[:], pos2)
+
+        slot_tokens = []
+        for q in range(E * C // GATHER):
+            lst = offs_sb[:, q * GATHER // 16:(q + 1) * GATHER // 16]
+            gs = keep.tile([P, GATHER], U8, name="gs%d" % q, align_bytes=64)
+            nc.vector.tensor_copy(out=gs[:], in_=xs[:].indirect(lst))
+            gw = []
+            for o in range(PASSES):
+                g = keep.tile([P, GATHER], U32, name="gw%d_%d" % (q, o), align_bytes=64)
+                nc.vector.tensor_copy(out=g[:], in_=xw[:, o * T:(o + 1) * T].bitcast(U32).indirect(lst))
+                gw.append(g)
+            for c0 in range(0, GATHER, C):
+                slot_tokens.append([(gw[o][:, c0:c0 + C], gs[4 * o:, c0:c0 + C]) for o in range(PASSES)])
+        all_tokens = [
+            [(xw[:, o * T + g * C:o * T + (g + 1) * C], xs[4 * o:, g * C:(g + 1) * C]) for o in range(PASSES)]
+            for g in range(T // C)
+        ]
+
+        ident = keep.tile([P, P], F32, name="ident")
+        make_identity(nc, ident[:])
+        gate_sb = []
+        for r in range(2):
+            bank = psum.tile([P, PACK, C], F32, name="abank", tag="abank", bufs=3)
+            for j in range(PACK):
+                nc.tensor.transpose(bank[:, j, :], gate_row[:, r, j:j + 1].to_broadcast([P, P]), ident[:])
+            g = keep.tile([P, P, PACK], F32, name="gate_sb%d" % r)
+            nc.scalar.copy(out=g[:], in_=bank[:].rearrange("p j n -> p n j"))
+            gate_sb.append(g)
+
+        def quantize_split(raw, o):
+            stage = stage_tile(o)
+            round_w("scalar", stage, 0, P // 2, raw, 0)
+            round_w("vector", stage, P // 2, P, raw, 0)
+            return quantize_w(stage, o), stage
+
+        y_slots = keep.tile([P, E * C], F32, name="y_slots")
+        steps = 2 * E
+        banks = {}
+        sig = {}
+        bank_y = {}
+        tail = {}
+
+        def load_step(s):
+            if s < steps - 1:
+                raws[s] = load_matrix((w1, w3)[s % 2][s // 2])
+            elif s == steps - 1:
+                raws[s] = [load_piece(w3[E - 1], o, 0, H) for o in range(PASSES)]
+            elif s == steps:
+                raws[s] = [load_piece(w1[E], o, 0, H) for o in range(PASSES)]
+            elif s == steps + 1:
+                raws[s] = [load_piece(w3[E], 0, 0, H), load_piece(w3[E], 1, 0, H // 2), load_piece(w3[E], 1, H // 2, H)]
+                tail["w2"] = raw_tile(PACK * N)
+                nc.sync.dma_start(out=tail["w2"][:], in_=w2[E].rearrange("(p j) n -> p (j n)", j=PACK))
+
+        def store_slots(e):
+            nc.scalar.copy(out=y_slots[:, e * C:(e + 1) * C], in_=bank_y[e][:])
+
+        for s in range(steps):
+            load_step(s + 3)
+            e = s // 2
+            if s < steps - 1:
+                stages = [stage_tile(o) for o in range(PASSES)]
+                round_w("scalar", stages[0], 0, P, raws[s][0], 0)
+                round_w("vector", stages[1], 0, P, raws[s][1], 0)
+                q_first = quantize_w(stages[1], 1)
+            else:
+                q_first = quantize_split(raws[s][0], 1)[0]
+            if s % 2 == 1:
+                sig[e] = sigmoid_of(banks[s - 1], raws[s][0][:, :H])
+            elif e > 0:
+                hidden = gated(banks[s - 1], sig[e - 1], stages[1][:, :H])
+                bank_y[e - 1] = second_layer(w2q, e - 1, quantize(hidden, C, "h", 4))
+                store_slots(e - 1)
+            if s < steps - 1:
+                wq = [quantize_w(stages[0], 0), q_first]
+            else:
+                wq = [q_first, quantize_split(raws[s][1], 0)[0]]
+            banks[s] = first_layer(wq, slot_tokens[e], ("abank", "bbank")[s % 2])
+            if s == 1:
+                stage2 = keep.tile([P, E * PACK * N], BF16, name="stage2", align_bytes=64)
+                half = E * PACK * N // 2
+                round_w2("scalar", stage2[:, :half], raw_w2[:, :half], E // 2)
+                round_w2("vector", stage2[:, half:], raw_w2[:, half:], E // 2)
+                w2q = quantize(stage2, E * N, "w2", 1, pieces=2)
+
+        raw_w1, raw_w3, raw_w2s = raws[steps], raws[steps + 1], tail["w2"]
+
+        def pick(lst, g, place):
+            nc.vector.tensor_tensor(
+                out=place, in0=y_slots[:].indirect(lst[:]), in1=g[:].rearrange("p n j -> p (n j)"), op=MULT
+            )
+            return place
+
+        q_first, stage = quantize_split(raw_w1[0], 1)
+        hidden = gated(banks[steps - 1], sig[E - 1], stage[:, :H])
+        bank_y[E - 1] = second_layer(w2q, E - 1, quantize(hidden, C, "h", 4))
+        store_slots(E - 1)
+        q1 = [q_first, quantize_split(raw_w1[1], 0)[0]]
+        first = pick(pos1_sb, gate_sb[0], raw_w1[1][:, :T])
+        banks_a = [first_layer(q1, all_tokens[g], "abank") for g in range(3)]
+        q3 = [quantize_split(raw_w3[0], 1)[0]]
+        second = pick(pos2_sb, gate_sb[1], raw_w3[0][:, H:H + T])
+        sigs = [sigmoid_of(banks_a[0], raw_w3[0][:, :H])]
+        banks_a.append(first_layer(q1, all_tokens[3], "abank"))
+        stage = ring.tile([P, PACK * H], BF16, name="stage_last", align_bytes=64)
+        round_w("scalar", stage, 0, P // 2, raw_w3[1], 0)
+        round_w("vector", stage, P // 2, P, raw_w3[2], P // 2)
+        q3.append(quantize(stage, H, "wlast", 1, pieces=4))
+        routed = raw_w3[2][:, H:H + T]
+        nc.vector.tensor_tensor(out=routed, in0=first, in1=second, op=ADD)
+        sigs.append(sigmoid_of(banks_a[1], raw_w3[1][:, :H]))
+        sigs.append(sigmoid_of(banks_a[2], raw_w3[1][:, H:]))
+        sigs.append(sigmoid_of(banks_a[3], raw_w3[2][:, :H]))
+        stage2s = keep.tile([P, PACK * N], BF16, name="stage2s", align_bytes=64)
+        round_w2("scalar", stage2s[:], raw_w2s[:], 1)
+
+        result = keep.tile([P, T], F32, name="result")
+        hidden = {}
+        hq = {}
+        groups = T // C
+        for step in range(groups + 2):
+            if step < groups:
+                place = ring.tile([P, H], BF16, name="hidden", tag="hidden", bufs=4, align_bytes=64)
+                hidden[step] = gated(first_layer(q3, all_tokens[step], "bbank"), sigs[step], place[:])
+            if step == 1:
+                w2sq = quantize(stage2s, N, "w2s", 1)
+            g = step - 1
+            if 0 <= g < groups:
+                hq[g] = second_layer(w2sq, 0, quantize(hidden[g], C, "h", 4))
+            g = step - 2
+            if 0 <= g < groups:
+                cols = slice(g * C, (g + 1) * C)
+                nc.vector.tensor_tensor(out=result[:, cols], in0=hq[g][:], in1=routed[:, cols], op=ADD)
+                nc.sync.dma_start(out=out[:, cols], in_=result[:, cols])

@@ -35,7 +35,7 @@ def tile_moe_shr_glu_sigmoid_kernel(
         psum = ctx.enter_context(tc.psum_pool(name="psum", bufs=1))
 
         def raw_tile(cols):
-            return ring.tile([P, cols], F32, name="raw", tag="raw", bufs=RAW_BUFS)
+            return ring.tile([P, cols], F32, name="raw", tag="raw", bufs=RAW_BUFS, align_bytes=64)
 
         def load_matrix(w):
             raw = raw_tile(PASSES * PACK * H)
@@ -61,10 +61,10 @@ def tile_moe_shr_glu_sigmoid_kernel(
                 nc.vector.tensor_copy(out=dst, in_=src)
 
         def stage_tile(o):
-            return ring.tile([P, PACK * H], BF16, name="stage%d" % o, tag="stage%d" % o, bufs=1, align_bytes=64)
+            return ring.tile([P, PACK * H], BF16, name="stage%d" % o, tag="stage%d" % o, bufs=2, align_bytes=64)
 
         def quantize_w(stage, o, pieces=1):
-            return quantize(stage, H, "w%d" % o, 1 + o, pieces)
+            return quantize(stage, H, "w%d" % o, 3, pieces)
 
         def round_w(engine, stage, m0, m1, raw, raw_m0):
             dst = stage[:].rearrange("p (t m j) -> p m j t", t=PACK, j=PACK)
@@ -194,11 +194,12 @@ def tile_moe_shr_glu_sigmoid_kernel(
             nc.scalar.copy(out=g[:], in_=bank[:].rearrange("p j n -> p n j"))
             gate_sb.append(g)
 
-        def quantize_split(raw, o):
+        def round_split(raw, o, cut):
             stage = stage_tile(o)
-            round_w("scalar", stage, 0, P // 2, raw, 0)
-            round_w("vector", stage, P // 2, P, raw, 0)
-            return quantize_w(stage, o), stage
+            round_w("scalar", stage, 0, cut, raw, 0)
+            if cut < P:
+                round_w("vector", stage, cut, P, raw, 0)
+            return stage
 
         y_slots = keep.tile([P, E * C], F32, name="y_slots")
         steps = 2 * E
@@ -231,7 +232,7 @@ def tile_moe_shr_glu_sigmoid_kernel(
                 round_w("vector", stages[1], 0, P, raws[s][1], 0)
                 q_first = quantize_w(stages[1], 1)
             else:
-                q_first = quantize_split(raws[s][0], 1)[0]
+                q_first = quantize_w(round_split(raws[s][0], 1, P // 2), 1)
             if s % 2 == 1:
                 sig[e] = sigmoid_of(banks[s - 1], raws[s][0][:, :H])
             elif e > 0:
@@ -241,7 +242,7 @@ def tile_moe_shr_glu_sigmoid_kernel(
             if s < steps - 1:
                 wq = [quantize_w(stages[0], 0), q_first]
             else:
-                wq = [q_first, quantize_split(raws[s][1], 0)[0]]
+                wq = [q_first, quantize_w(round_split(raws[s][1], 0, 44), 0, pieces=4)]
             banks[s] = first_layer(wq, slot_tokens[e], ("abank", "bbank")[s % 2])
             if s == 1:
                 stage2 = keep.tile([P, E * PACK * N], BF16, name="stage2", align_bytes=64)
@@ -258,26 +259,28 @@ def tile_moe_shr_glu_sigmoid_kernel(
             )
             return place
 
-        q_first, stage = quantize_split(raw_w1[0], 1)
-        hidden = gated(banks[steps - 1], sig[E - 1], stage[:, :H])
+        stage = round_split(raw_w1[0], 1, P // 2)
+        hidden = gated(banks[steps - 1], sig[E - 1], raw_w1[0][:, :H // 2].bitcast(BF16))
+        q_first = quantize_w(stage, 1)
         bank_y[E - 1] = second_layer(w2q, E - 1, quantize(hidden, C, "h", 4))
         store_slots(E - 1)
-        q1 = [q_first, quantize_split(raw_w1[1], 0)[0]]
+        q1 = [q_first, quantize_w(round_split(raw_w1[1], 0, P // 2), 0)]
         first = pick(pos1_sb, gate_sb[0], raw_w1[1][:, :T])
+        second = pick(pos2_sb, gate_sb[1], raw_w1[1][:, T:2 * T])
         banks_a = [first_layer(q1, all_tokens[g], "abank") for g in range(3)]
-        q3 = [quantize_split(raw_w3[0], 1)[0]]
-        second = pick(pos2_sb, gate_sb[1], raw_w3[0][:, H:H + T])
-        sigs = [sigmoid_of(banks_a[0], raw_w3[0][:, :H])]
-        banks_a.append(first_layer(q1, all_tokens[3], "abank"))
+        q3 = [quantize_w(round_split(raw_w3[0], 1, P), 1)]
         stage = ring.tile([P, PACK * H], BF16, name="stage_last", align_bytes=64)
         round_w("scalar", stage, 0, P // 2, raw_w3[1], 0)
         round_w("vector", stage, P // 2, P, raw_w3[2], P // 2)
         q3.append(quantize(stage, H, "wlast", 1, pieces=4))
         routed = raw_w3[2][:, H:H + T]
         nc.vector.tensor_tensor(out=routed, in0=first, in1=second, op=ADD)
-        sigs.append(sigmoid_of(banks_a[1], raw_w3[1][:, :H]))
-        sigs.append(sigmoid_of(banks_a[2], raw_w3[1][:, H:]))
-        sigs.append(sigmoid_of(banks_a[3], raw_w3[2][:, :H]))
+        sigs = [sigmoid_of(banks_a[0], raw_w3[1][:, :H])]
+        sigs.append(sigmoid_of(banks_a[1], raw_w3[1][:, H:]))
+        sigs.append(sigmoid_of(banks_a[2], raw_w3[2][:, :H]))
+        banks_a.append(first_layer(q1, all_tokens[3], "abank"))
+        sig_last = keep.tile([P, H], F32, name="sig_last")
+        sigs.append(sigmoid_of(banks_a[3], sig_last[:]))
         stage2s = keep.tile([P, PACK * N], BF16, name="stage2s", align_bytes=64)
         round_w2("scalar", stage2s[:], raw_w2s[:], 1)
 

from contextlib import ExitStack

import concourse.mybir as mybir
from concourse.masks import make_identity

K, T, E, C, H, N = 1024, 512, 8, 128, 512, 128
FLOPS = 3422552064

F32 = mybir.dt.float32
BF16 = mybir.dt.bfloat16
I32 = mybir.dt.int32
U32 = mybir.dt.uint32
U16 = mybir.dt.uint16
U8 = mybir.dt.uint8
FP8X4 = mybir.dt.float8_e4m3fn_x4
MULT = mybir.AluOpType.mult
ADD = mybir.AluOpType.add
SIGMOID = mybir.ActivationFunctionType.Sigmoid

P = 128
PACK = 4
K_PASS = P * PACK
PASSES = K // K_PASS
GATHER = 256
RAW_BUFS = 8


def tile_moe_shr_glu_sigmoid_kernel(
    tc, x_words, x_scales, w1, w3, w2, gate, offs, pos1, pos2, out
):
    nc = tc.nc
    with ExitStack() as ctx:
        keep = ctx.enter_context(tc.tile_pool(name="keep", bufs=1))
        ring = ctx.enter_context(tc.tile_pool(name="ring", bufs=1))
        psum = ctx.enter_context(tc.psum_pool(name="psum", bufs=1))

        def raw_tile(cols):
            return ring.tile([P, cols], F32, name="raw", tag="raw", bufs=RAW_BUFS, align_bytes=64)

        def load_matrix(w):
            raw = raw_tile(PASSES * PACK * H)
            nc.sync.dma_start(
                out=raw[:].rearrange("p (o r) -> p o r", o=PASSES),
                in_=w.rearrange("(o p j) c -> p o (j c)", o=PASSES, j=PACK),
            )
            return [raw[:, o * PACK * H:(o + 1) * PACK * H] for o in range(PASSES)]

        def load_piece(w, o, c0, c1):
            raw = raw_tile(PACK * (c1 - c0))
            rows = w[o * K_PASS:(o + 1) * K_PASS, c0:c1]
            nc.sync.dma_start(
                out=raw[:].rearrange("p (j c) -> p j c", j=PACK),
                in_=rows.rearrange("(p j) c -> p j c", j=PACK),
            )
            return raw[:]

        def copy_on(engine, dst, src):
            if engine == "scalar":
                nc.scalar.copy(out=dst, in_=src)
            else:
                nc.vector.tensor_copy(out=dst, in_=src)

        def stage_tile(o):
            return ring.tile([P, PACK * H], BF16, name="stage%d" % o, tag="stage%d" % o, bufs=2, align_bytes=64)

        def quantize_w(stage, o, pieces=1):
            return quantize(stage, H, "w%d" % o, 3, pieces)

        def round_w(engine, stage, m0, m1, raw, raw_m0):
            dst = stage[:].rearrange("p (t m j) -> p m j t", t=PACK, j=PACK)
            src = raw.rearrange("p (j m t) -> p m j t", j=PACK, t=PACK)
            copy_on(engine, dst[:, m0:m1], src[:, m0 - raw_m0:m1 - raw_m0])

        def quantize(stage, words, tag, bufs, pieces=1):
            codes = ring.tile([P, words], U32, name=tag + "_codes", tag=tag + "_codes", bufs=bufs, align_bytes=64)
            scales = ring.tile([P, words], U8, name=tag + "_scales", tag=tag + "_scales", bufs=bufs, align_bytes=64)
            step = words // pieces
            for i in range(pieces):
                nc.vector.quantize_mx(
                    out=codes[:, i * step:(i + 1) * step].bitcast(FP8X4),
                    scales=scales[:, i * step:(i + 1) * step],
                    in_=stage[:, PACK * i * step:PACK * (i + 1) * step],
                )
            return codes, scales

        def round_w2(engine, stage, raw, experts):
            dst = stage.rearrange("p (e c i j) -> p e c j i", e=experts, i=4, j=PACK)
            src = raw.rearrange("p (e j c i) -> p e c j i", e=experts, j=PACK, i=4)
            copy_on(engine, dst, src)

        def first_layer(wq, tokens, tag):
            bank = psum.tile([P, PACK, C], F32, name=tag, tag=tag, bufs=3)
            for t in range(PACK):
                cols = slice(t * P, (t + 1) * P)
                for o in range(PASSES):
                    codes, scales = wq[o]
                    words, bytes_ = tokens[o]
                    nc.tensor.matmul_mx(
                        out=bank[:, t, :],
                        lhsT=codes[:, cols].bitcast(FP8X4),
                        lhsT_scale=scales[:, cols],
                        rhs=words.bitcast(FP8X4),
                        rhs_scale=bytes_,
                        start=(o == 0),
                        stop=(o == PASSES - 1),
                    )
            return bank

        def sigmoid_of(bank, place):
            sig = place.rearrange("p (n t) -> p n t", t=PACK)
            nc.scalar.activation(out=sig, in_=bank[:].rearrange("p t n -> p n t"), func=SIGMOID)
            return sig

        def gated(bank, sig, hidden):
            nc.vector.tensor_tensor(
                out=hidden.rearrange("p (n t) -> p n t", t=PACK),
                in0=bank[:].rearrange("p t n -> p n t"),
                in1=sig,
                op=MULT,
            )
            return hidden

        def second_layer(w2q, e, hq):
            bank = psum.tile([P, C], F32, name="ybank", tag="ybank", bufs=2)
            cols = slice(e * N, (e + 1) * N)
            nc.tensor.matmul_mx(
                out=bank[:],
                lhsT=w2q[0][:, cols].bitcast(FP8X4),
                lhsT_scale=w2q[1][:, cols],
                rhs=hq[0][:].bitcast(FP8X4),
                rhs_scale=hq[1][:],
                start=True,
                stop=True,
            )
            return bank

        xs = keep.tile([P, T], U8, name="xs", align_bytes=64)
        nc.vector.memset(xs[:].bitcast(I32), 0)
        xw = keep.tile([P, PASSES * T], I32, name="xw", align_bytes=64)
        nc.sync.dma_start(
            out=xw[:].rearrange("p (o t) -> p o t", o=PASSES),
            in_=x_words.rearrange("o p t r -> p o (t r)").bitcast(I32),
        )
        offs_sb = keep.tile([P, E * C // 16], U16, name="offs_sb")
        nc.sync.dma_start(offs_sb[:], offs)
        xs_rows = keep.tile([P, T // 4], I32, name="xs_rows")
        for q in range(4):
            nc.sync.dma_start(
                out=xs_rows[32 * q:32 * q + 4 * PASSES, :],
                in_=x_scales[:, 4 * q:4 * q + 4, :].bitcast(I32),
            )
        gate_row = keep.tile([P, 2, PACK], F32, name="gate_row")
        nc.sync.dma_start(out=gate_row[:], in_=gate[:, 0, :].rearrange("r (p j) -> p r j", j=PACK))
        raws = {0: load_matrix(w1[0]), 1: load_matrix(w3[0])}
        for q in range(4):
            rows = slice(32 * q, 32 * q + 4 * PASSES)
            nc.vector.tensor_copy(out=xs[:].bitcast(I32)[rows, :], in_=xs_rows[rows, :])
        raw_w2 = raw_tile(E * PACK * N)
        nc.sync.dma_start(
            out=raw_w2[:].rearrange("p (e r) -> p e r", e=E),
            in_=w2[0:E].rearrange("e (p j) n -> p e (j n)", j=PACK),
        )
        raws[2] = load_matrix(w1[1])
        pos1_sb = keep.tile([P, T // 16], U16, name="pos1_sb")
        nc.sync.dma_start(pos1_sb[:], pos1)
        pos2_sb = keep.tile([P, T // 16], U16, name="pos2_sb")
        nc.sync.dma_start(pos2_sb[:], pos2)

        slot_tokens = []
        for q in range(E * C // GATHER):
            lst = offs_sb[:, q * GATHER // 16:(q + 1) * GATHER // 16]
            gs = keep.tile([P, GATHER], U8, name="gs%d" % q, align_bytes=64)
            nc.vector.tensor_copy(out=gs[:], in_=xs[:].indirect(lst))
            gw = []
            for o in range(PASSES):
                g = keep.tile([P, GATHER], U32, name="gw%d_%d" % (q, o), align_bytes=64)
                nc.vector.tensor_copy(out=g[:], in_=xw[:, o * T:(o + 1) * T].bitcast(U32).indirect(lst))
                gw.append(g)
            for c0 in range(0, GATHER, C):
                slot_tokens.append([(gw[o][:, c0:c0 + C], gs[4 * o:, c0:c0 + C]) for o in range(PASSES)])
        all_tokens = [
            [(xw[:, o * T + g * C:o * T + (g + 1) * C], xs[4 * o:, g * C:(g + 1) * C]) for o in range(PASSES)]
            for g in range(T // C)
        ]

        ident = keep.tile([P, P], F32, name="ident")
        make_identity(nc, ident[:])
        gate_sb = []
        for r in range(2):
            bank = psum.tile([P, PACK, C], F32, name="abank", tag="abank", bufs=3)
            for j in range(PACK):
                nc.tensor.transpose(bank[:, j, :], gate_row[:, r, j:j + 1].to_broadcast([P, P]), ident[:])
            g = keep.tile([P, P, PACK], F32, name="gate_sb%d" % r)
            nc.scalar.copy(out=g[:], in_=bank[:].rearrange("p j n -> p n j"))
            gate_sb.append(g)

        def round_split(raw, o, cut):
            stage = stage_tile(o)
            round_w("scalar", stage, 0, cut, raw, 0)
            if cut < P:
                round_w("vector", stage, cut, P, raw, 0)
            return stage

        y_slots = keep.tile([P, E * C], F32, name="y_slots")
        steps = 2 * E
        banks = {}
        sig = {}
        bank_y = {}
        tail = {}

        def load_step(s):
            if s < steps - 1:
                raws[s] = load_matrix((w1, w3)[s % 2][s // 2])
            elif s == steps - 1:
                raws[s] = [load_piece(w3[E - 1], o, 0, H) for o in range(PASSES)]
            elif s == steps:
                raws[s] = [load_piece(w1[E], o, 0, H) for o in range(PASSES)]
            elif s == steps + 1:
                raws[s] = [load_piece(w3[E], 0, 0, H), load_piece(w3[E], 1, 0, H // 2), load_piece(w3[E], 1, H // 2, H)]
                tail["w2"] = raw_tile(PACK * N)
                nc.sync.dma_start(out=tail["w2"][:], in_=w2[E].rearrange("(p j) n -> p (j n)", j=PACK))

        def store_slots(e):
            nc.scalar.copy(out=y_slots[:, e * C:(e + 1) * C], in_=bank_y[e][:])

        for s in range(steps):
            load_step(s + 3)
            e = s // 2
            if s < steps - 1:
                stages = [stage_tile(o) for o in range(PASSES)]
                round_w("scalar", stages[0], 0, P, raws[s][0], 0)
                round_w("vector", stages[1], 0, P, raws[s][1], 0)
                q_first = quantize_w(stages[1], 1)
            else:
                q_first = quantize_w(round_split(raws[s][0], 1, P // 2), 1)
            if s % 2 == 1:
                sig[e] = sigmoid_of(banks[s - 1], raws[s][0][:, :H])
            elif e > 0:
                hidden = gated(banks[s - 1], sig[e - 1], stages[1][:, :H])
                bank_y[e - 1] = second_layer(w2q, e - 1, quantize(hidden, C, "h", 4))
                store_slots(e - 1)
            if s < steps - 1:
                wq = [quantize_w(stages[0], 0), q_first]
            else:
                wq = [q_first, quantize_w(round_split(raws[s][1], 0, 44), 0, pieces=4)]
            banks[s] = first_layer(wq, slot_tokens[e], ("abank", "bbank")[s % 2])
            if s == 1:
                stage2 = keep.tile([P, E * PACK * N], BF16, name="stage2", align_bytes=64)
                half = E * PACK * N // 2
                round_w2("scalar", stage2[:, :half], raw_w2[:, :half], E // 2)
                round_w2("vector", stage2[:, half:], raw_w2[:, half:], E // 2)
                w2q = quantize(stage2, E * N, "w2", 1, pieces=2)

        raw_w1, raw_w3, raw_w2s = raws[steps], raws[steps + 1], tail["w2"]

        def pick(lst, g, place):
            nc.vector.tensor_tensor(
                out=place, in0=y_slots[:].indirect(lst[:]), in1=g[:].rearrange("p n j -> p (n j)"), op=MULT
            )
            return place

        stage = round_split(raw_w1[0], 1, P // 2)
        hidden = gated(banks[steps - 1], sig[E - 1], raw_w1[0][:, :H // 2].bitcast(BF16))
        q_first = quantize_w(stage, 1)
        bank_y[E - 1] = second_layer(w2q, E - 1, quantize(hidden, C, "h", 4))
        store_slots(E - 1)
        q1 = [q_first, quantize_w(round_split(raw_w1[1], 0, P // 2), 0)]
        first = pick(pos1_sb, gate_sb[0], raw_w1[1][:, :T])
        second = pick(pos2_sb, gate_sb[1], raw_w1[1][:, T:2 * T])
        banks_a = [first_layer(q1, all_tokens[g], "abank") for g in range(3)]
        q3 = [quantize_w(round_split(raw_w3[0], 1, P), 1)]
        stage = ring.tile([P, PACK * H], BF16, name="stage_last", align_bytes=64)
        round_w("scalar", stage, 0, P // 2, raw_w3[1], 0)
        round_w("vector", stage, P // 2, P, raw_w3[2], P // 2)
        q3.append(quantize(stage, H, "wlast", 1, pieces=4))
        routed = raw_w3[2][:, H:H + T]
        nc.vector.tensor_tensor(out=routed, in0=first, in1=second, op=ADD)
        sigs = [sigmoid_of(banks_a[0], raw_w3[1][:, :H])]
        sigs.append(sigmoid_of(banks_a[1], raw_w3[1][:, H:]))
        sigs.append(sigmoid_of(banks_a[2], raw_w3[2][:, :H]))
        banks_a.append(first_layer(q1, all_tokens[3], "abank"))
        sig_last = keep.tile([P, H], F32, name="sig_last")
        sigs.append(sigmoid_of(banks_a[3], sig_last[:]))
        stage2s = keep.tile([P, PACK * N], BF16, name="stage2s", align_bytes=64)
        round_w2("scalar", stage2s[:], raw_w2s[:], 1)

        result = keep.tile([P, T], F32, name="result")
        hidden = {}
        hq = {}
        groups = T // C
        for step in range(groups + 2):
            if step < groups:
                place = ring.tile([P, H], BF16, name="hidden", tag="hidden", bufs=4, align_bytes=64)
                hidden[step] = gated(first_layer(q3, all_tokens[step], "bbank"), sigs[step], place[:])
            if step == 1:
                w2sq = quantize(stage2s, N, "w2s", 1)
            g = step - 1
            if 0 <= g < groups:
                hq[g] = second_layer(w2sq, 0, quantize(hidden[g], C, "h", 4))
            g = step - 2
            if 0 <= g < groups:
                cols = slice(g * C, (g + 1) * C)
                nc.vector.tensor_tensor(out=result[:, cols], in0=hq[g][:], in1=routed[:, cols], op=ADD)
                nc.sync.dma_start(out=out[:, cols], in_=result[:, cols])
